import numpy as np
import ml_dtypes


def mxq(x, axis, fmt="e4m3"):
    dtype, down = {"e4m3": (ml_dtypes.float8_e4m3fn, 7), "e5m2": (ml_dtypes.float8_e5m2, 14)}[fmt]
    v = np.moveaxis(np.asarray(x, np.float32).astype(ml_dtypes.bfloat16).astype(np.float64), axis, -1)
    blocks = v.reshape(v.shape[:-1] + (-1, 32))
    amax = np.abs(blocks).max(-1, keepdims=True)
    byte = np.maximum(np.where(amax > 0, np.frexp(amax)[1] - 1 + 127, 0) - down, 1)
    scale = np.exp2(byte - 127.0)
    codes = (blocks / scale).astype(np.float32).astype(dtype).astype(np.float64)
    return np.moveaxis((codes * scale).reshape(v.shape), -1, axis)


WIDE = False


def mx_kscale(k):
    if not WIDE:
        return np.ones(k)
    levels = np.array([30, -30])
    if k % 512:
        return np.exp2(np.random.permutation(np.resize(levels, k // 32))).repeat(32)
    a = np.empty((k // 512, 16))
    for p in range(k // 512):
        a[p, :8] = np.random.permutation(np.resize(levels, 8))
        for g in range(8):
            far = levels[np.abs(levels - a[p, g]) >= 10]
            a[p, g + 8] = far[np.random.randint(len(far))]
    return np.exp2(a.ravel()).repeat(32)


def f64(x):
    return np.asarray(x).astype(np.float64)


def striped(idx):
    return np.tile(np.asarray(idx).reshape(-1, 16).T, (8, 1)).astype(np.uint16)


def unstriped(offs):
    return offs[:16].T.reshape(-1).astype(np.int64)


E2M1 = np.array([0.0, 0.5, 1.0, 1.5, 2.0, 3.0, 4.0, 6.0, -0.0, -0.5, -1.0, -1.5, -2.0, -3.0, -4.0, -6.0])


def pack_weight(w, fmt):
    k, n = w.shape
    w = f64(np.asarray(w, np.float32).astype(ml_dtypes.bfloat16)).reshape(k // 32, 32, n)
    amax = np.abs(w).max(1)
    if fmt in ("e4m3", "e5m2"):
        byte = np.frexp(amax)[1] - 1 + 127 - (7 if fmt == "e4m3" else 14)
    else:
        mant, ex = np.frexp(amax / 6.0)
        byte = np.where(mant > 0.5, ex, ex - 1) + 127
    byte = np.clip(np.where(amax > 0, byte, 1), 1, 254)
    scaled = (w * np.exp2(127.0 - byte)[:, None, :]).reshape(k, n).astype(np.float32)
    by_word = np.ascontiguousarray(scaled.reshape(k // 512, 128, 4, n).transpose(0, 1, 3, 2))
    if fmt in ("e4m3", "e5m2"):
        words = by_word.astype(ml_dtypes.float8_e4m3fn if fmt == "e4m3" else ml_dtypes.float8_e5m2).view(np.uint8)
    else:
        c = by_word.astype(ml_dtypes.float4_e2m1fn).view(np.uint8) & 0xF
        words = (c[..., 0::2] | (c[..., 1::2] << 4)).reshape(k // 512, 128, 2 * n)
    return np.ascontiguousarray(words), np.ascontiguousarray(byte.astype(np.uint8).reshape(k // 512, 16, n))


def unpack_weight(words, scales, fmt):
    g, _, n = scales.shape
    words = np.ascontiguousarray(words).reshape(g, 128, n, -1)
    if fmt in ("e4m3", "e5m2"):
        vals = words.view(ml_dtypes.float8_e4m3fn if fmt == "e4m3" else ml_dtypes.float8_e5m2).astype(np.float64)
    else:
        nib = np.empty((g, 128, n, 4), np.uint8)
        nib[..., 0::2] = words & 0xF
        nib[..., 1::2] = words >> 4
        vals = E2M1[nib]
    vals = vals * np.repeat(np.exp2(scales.astype(np.float64) - 127.0), 8, axis=1)[..., None]
    return vals.transpose(0, 1, 3, 2).reshape(g * 512, n)


K, T, J, I, L, S, R, F, Z, N = 512, 512, 256, 128, 128, 512, 512, 512, 1024, 256


def setup_inputs():
    n = np.random.standard_normal
    idx = np.random.permutation(T)[:I]
    idx2 = np.random.permutation(S)[:L]
    idx3 = np.random.permutation(Z)[:J]
    fk = mx_kscale(K)
    fr = mx_kscale(R)
    ff = mx_kscale(F)
    wp = pack_weight(n((K, R)) * 1 / np.sqrt(K) * fk[:, None] * fr, "e5m2")
    w2p = pack_weight(n((F, R)) * 1 / np.sqrt(F) * ff[:, None] * fr, "e5m2")
    wbp = pack_weight(n((R, N)) * 1 / np.sqrt(R) / fr[:, None], "e4m3")
    return {
        "xa": (n((K, T)) / fk[:, None]).astype(np.float32),
        "xb": (n((K, S)) * 0.6 / fk[:, None]).astype(np.float32),
        "w_words": wp[0],
        "w_scales": wp[1],
        "xo": (n((F, Z))).astype(np.float32),
        "fl": (np.random.uniform(0.5, 2.0, (F, 1)) / ff[:, None]).astype(np.float32),
        "so": (n((F, J)) * 0.8).astype(np.float32),
        "w2_words": w2p[0],
        "w2_scales": w2p[1],
        "wb_words": wbp[0],
        "wb_scales": wbp[1],
        "rs": (1.0 * n((J, N))).astype(np.float32),
        "offs": striped(idx),
        "offs2": striped(idx2),
        "offs3": striped(idx3),
    }


def reference(xa, xb, w_words, w_scales, xo, fl, so, w2_words, w2_scales, wb_words, wb_scales, rs, offs, offs2, offs3):
    idx = unstriped(offs)
    idx2 = unstriped(offs2)
    idx3 = unstriped(offs3)
    wu = unpack_weight(w_words, w_scales, "e5m2")
    w2u = unpack_weight(w2_words, w2_scales, "e5m2")
    wbu = unpack_weight(wb_words, wb_scales, "e4m3")
    u = np.concatenate([f64(xa)[:, idx], f64(xb)[:, idx2]], axis=1)
    u2 = np.maximum(f64(xo)[:, idx3], f64(so)) * f64(fl)
    uq = mxq(u, 0, "e5m2")
    a = wu.T @ uq
    u2q = mxq(u2, 0, "e4m3")
    q = w2u.T @ u2q
    hid = np.abs(a - q)
    hidq = mxq(hid, 0, "e5m2")
    p = hidq.T @ wbu
    pk2 = np.max(np.abs(p), axis=1, keepdims=True)
    y = p / (pk2 + 0.2) + 0.3 * f64(rs)
    return y

@@ -1,0 +1,259 @@
+from contextlib import ExitStack
+
+import concourse.mybir as mybir
+
+K, T, J, R, Z, N = 512, 512, 256, 512, 1024, 256
+FLOPS = 2 * K * R * J * 2 + 2 * J * R * N
+
+F32 = mybir.dt.float32
+BF16 = mybir.dt.bfloat16
+I32 = mybir.dt.int32
+U32 = mybir.dt.uint32
+U16 = mybir.dt.uint16
+U8 = mybir.dt.uint8
+E4M3 = mybir.dt.float8_e4m3fn_x4
+E5M2 = mybir.dt.float8_e5m2_x4
+ALU = mybir.AluOpType
+ACT = mybir.ActivationFunctionType
+
+P = 128
+PACK = 4
+H = 128
+
+
+def tile_list_two_joined_largest_absgap_rowpeaks_kernel(
+    tc, xa, xb, w_words, w_scales, xo, fl, so, w2_words, w2_scales, wb_words, wb_scales, rs, offs, offs2, offs3, out
+):
+    nc = tc.nc
+    with ExitStack() as ctx:
+        sb = ctx.enter_context(tc.tile_pool(name="sb", bufs=1))
+        ps = ctx.enter_context(tc.psum_pool(name="ps", bufs=1))
+
+        def tile(shape, dtype, name):
+            return sb.tile(shape, dtype, name=name, align_bytes=64)
+
+        lists = [tile([P, 8], U16, "list_a"), tile([P, 8], U16, "list_b")]
+        list_o = tile([P, 16], U16, "list_o")
+        fl_t = tile([P, PACK], F32, "fl_t")
+        so_t = tile([P, PACK * J], F32, "so_t")
+        xo_t = [tile([P, Z], F32, "xo%d" % t) for t in range(PACK)]
+        front = [tile([P, 2 * T], F32, "front%d" % h) for h in range(2)]
+        back = [[tile([P, T], F32, "back%d_%d" % (h, t)) for t in range(2)] for h in range(2)]
+        raw_words = {n: tile([P, R], U32, "raw_words_" + n) for n in ("w", "w2")}
+        raw_scales = {n: tile([P, R], U8, "raw_scales_" + n) for n in ("w", "w2")}
+        words = {n: tile([P, R], U32, "words_" + n) for n in ("w", "w2")}
+        scales = {n: tile([P, R], U8, "scales_" + n) for n in ("w", "w2")}
+        wb_w = tile([P, N], U32, "wb_w")
+        wb_s = tile([P, N], U8, "wb_s")
+        rs_t = tile([P, 2 * N], F32, "rs_t")
+
+        for plane in (raw_scales["w2"], raw_scales["w"], wb_s):
+            nc.vector.memset(plane[:].bitcast(I32), 0)
+
+        def load(dst, src):
+            nc.sync.dma_start(out=dst, in_=src)
+
+        def load_words(dst, src):
+            load(dst[:].bitcast(I32), src[0].rearrange("p n t -> p (n t)").bitcast(I32))
+
+        def load_scales(dst, src, quadrants):
+            for q in quadrants:
+                load(dst[32 * q : 32 * q + 4, :].bitcast(I32), src[0, 4 * q : 4 * q + 4, :].bitcast(I32))
+
+        def planes(x):
+            return x.rearrange("(p t) c -> p (t c)", t=PACK)
+
+        def load_front(h):
+            load(front[h][:], planes((xa, xb)[h])[:, 0 : 2 * T])
+
+        def load_back(h, t):
+            load(back[h][t][:], planes((xa, xb)[h])[:, (2 + t) * T : (3 + t) * T])
+
+        def load_xo(t):
+            load(xo_t[t][:], planes(xo)[:, t * Z : (t + 1) * Z])
+
+        load(so_t[:], planes(so))
+        load_xo(0)
+        load(list_o[:], offs3)
+        load(fl_t[:], planes(fl))
+        load_words(raw_words["w2"], w2_words)
+        load_scales(raw_scales["w2"], w2_scales, (0, 1))
+        load_xo(1)
+        load_scales(raw_scales["w2"], w2_scales, (2, 3))
+        load_words(raw_words["w"], w_words)
+        load_scales(raw_scales["w"], w_scales, (0, 1))
+        load_xo(2)
+        load_scales(raw_scales["w"], w_scales, (2, 3))
+        load_xo(3)
+        load(lists[0][:], offs)
+        load(lists[1][:], offs2)
+        load_front(0)
+        load_scales(wb_s, wb_scales, (0, 1))
+        load_back(0, 0)
+        load_scales(wb_s, wb_scales, (2, 3))
+        load_back(0, 1)
+        load_front(1)
+        load_back(1, 0)
+        load_back(1, 1)
+        load_words(wb_w, wb_words)
+        load(rs_t[:].rearrange("p (h n) -> p h n", h=2), rs.rearrange("(h p) n -> p h n", h=2))
+
+        def deal(n):
+            nc.vector.tensor_copy(
+                out=words[n][:].rearrange("p (t a i) -> p a t i", t=PACK, i=4),
+                in_=raw_words[n][:].rearrange("p (a i t) -> p a t i", t=PACK, i=4),
+            )
+            nc.vector.tensor_copy(
+                out=scales[n][:].rearrange("p (t a i) -> p a t i", t=PACK, i=16),
+                in_=raw_scales[n][:].rearrange("p (a i t) -> p a t i", t=PACK, i=16),
+            )
+
+        u2 = tile([P, J, PACK], BF16, "u2")
+
+        def side_plane(t):
+            picked = tile([P, J], F32, "picked_o%d" % t)
+            nc.scalar.activation(out=picked[:], in_=xo_t[t][:].indirect(list_o[:]), func=ACT.Copy)
+            larger = tile([P, J], F32, "larger%d" % t)
+            nc.vector.tensor_tensor(out=larger[:], in0=picked[:], in1=so_t[:, t * J : (t + 1) * J], op=ALU.max)
+            nc.vector.tensor_scalar(
+                out=u2[:, :, t], in0=larger[:], scalar1=fl_t[:, t : t + 1], scalar2=-1.0, op0=ALU.mult, op1=ALU.mult
+            )
+
+        side_plane(0)
+        deal("w2")
+        side_plane(1)
+        deal("w")
+        side_plane(2)
+        side_plane(3)
+
+        u2_w = tile([P, J], U32, "u2_w")
+        u2_s = tile([P, J], U8, "u2_s")
+        nc.vector.quantize_mx(out=u2_w[:].bitcast(E4M3), scales=u2_s[:], in_=u2[:].rearrange("p j t -> p (j t)"))
+
+        gap = [ps.tile([P, PACK, H], F32, name="gap%d" % h) for h in range(2)]
+        for h in range(2):
+            for t in range(PACK):
+                nc.tensor.matmul_mx(
+                    out=gap[h][:, t, :],
+                    lhsT=words["w2"][:, t * P : (t + 1) * P].bitcast(E5M2),
+                    lhsT_scale=scales["w2"][:, t * P : (t + 1) * P],
+                    rhs=u2_w[:, h * H : (h + 1) * H].bitcast(E4M3),
+                    rhs_scale=u2_s[:, h * H : (h + 1) * H],
+                    start=(t == 0),
+                    stop=False,
+                )
+
+        u = [tile([P, H, PACK], BF16, "u%d" % h) for h in range(2)]
+        picked = [tile([P, 2, H], F32, "picked%d" % h) for h in range(2)]
+        u_w = [tile([P, H], U32, "u_w%d" % h) for h in range(2)]
+        u_s = [tile([P, H], U8, "u_s%d" % h) for h in range(2)]
+        hid = [tile([P, H, PACK], BF16, "hid%d" % h) for h in range(2)]
+        hid_w = [tile([P, H], U32, "hid_w%d" % h) for h in range(2)]
+        hid_s = [tile([P, H], U8, "hid_s%d" % h) for h in range(2)]
+        prod = [ps.tile([P, N], F32, name="prod%d" % h) for h in range(2)]
+        resid = [tile([P, N], F32, "resid%d" % h) for h in range(2)]
+        size = [tile([P, N], F32, "size%d" % h) for h in range(2)]
+        lifted = [tile([P, N], F32, "lifted%d" % h) for h in range(2)]
+        denom = [tile([P, 1], F32, "denom%d" % h) for h in range(2)]
+        inv = [tile([P, 1], F32, "inv%d" % h) for h in range(2)]
+        res = [tile([P, N], F32, "res%d" % h) for h in range(2)]
+
+        def pick_front(h):
+            for t in range(2):
+                nc.scalar.activation(
+                    out=picked[h][:, t, :], in_=front[h][:, t * T : (t + 1) * T].indirect(lists[h][:]), func=ACT.Copy
+                )
+
+        def weave_front(h):
+            nc.vector.tensor_copy(out=u[h][:, :, 0:2], in_=picked[h][:].rearrange("p t j -> p j t"))
+
+        def pick_back(h, t):
+            nc.vector.tensor_copy(out=u[h][:, :, 2 + t], in_=back[h][t][:].indirect(lists[h][:]))
+
+        def quantise_u(h):
+            nc.vector.quantize_mx(
+                out=u_w[h][:].bitcast(E5M2), scales=u_s[h][:], in_=u[h][:].rearrange("p j t -> p (j t)")
+            )
+
+        def first_product(h):
+            for t in range(PACK):
+                nc.tensor.matmul_mx(
+                    out=gap[h][:, t, :],
+                    lhsT=words["w"][:, t * P : (t + 1) * P].bitcast(E5M2),
+                    lhsT_scale=scales["w"][:, t * P : (t + 1) * P],
+                    rhs=u_w[h][:].bitcast(E5M2),
+                    rhs_scale=u_s[h][:],
+                    start=False,
+                    stop=(t == PACK - 1),
+                )
+
+        def magnitude(h):
+            nc.scalar.activation(out=hid[h][:], in_=gap[h][:].rearrange("p t j -> p j t"), func=ACT.Abs)
+
+        def quantise_hid(h):
+            nc.vector.quantize_mx(
+                out=hid_w[h][:].bitcast(E5M2), scales=hid_s[h][:], in_=hid[h][:].rearrange("p j t -> p (j t)")
+            )
+
+        def second_product(h):
+            nc.tensor.matmul_mx(
+                out=prod[h][:],
+                lhsT=hid_w[h][:].bitcast(E5M2),
+                lhsT_scale=hid_s[h][:],
+                rhs=wb_w[:].bitcast(E4M3),
+                rhs_scale=wb_s[:],
+                start=True,
+                stop=True,
+            )
+
+        def scale_residual(h):
+            nc.vector.tensor_scalar(
+                out=resid[h][:], in0=rs_t[:, h * N : (h + 1) * N], scalar1=0.3, scalar2=None, op0=ALU.mult
+            )
+
+        def row_sizes(h):
+            nc.scalar.activation(out=size[h][:], in_=prod[h][:], func=ACT.Abs)
+
+        def row_peak(h):
+            nc.vector.tensor_scalar(
+                out=lifted[h][:], in0=size[h][:], scalar1=0.2, scalar2=None, op0=ALU.add, op1=ALU.max,
+                accum_out=denom[h][:],
+            )
+
+        def invert(h):
+            nc.vector.reciprocal(out=inv[h][:], in_=denom[h][:])
+
+        def finish(h):
+            nc.vector.scalar_tensor_tensor(
+                out=res[h][:], in0=prod[h][:], scalar=inv[h][:], in1=resid[h][:], op0=ALU.mult, op1=ALU.add
+            )
+            nc.sync.dma_start(out=out[h * H : (h + 1) * H, :], in_=res[h][:])
+
+        pick_front(0)
+        weave_front(0)
+        pick_back(0, 0)
+        pick_back(0, 1)
+        quantise_u(0)
+        first_product(0)
+        pick_front(1)
+        magnitude(0)
+        pick_back(1, 0)
+        weave_front(1)
+        pick_back(1, 1)
+        quantise_hid(0)
+        quantise_u(1)
+        second_product(0)
+        first_product(1)
+        row_sizes(0)
+        magnitude(1)
+        scale_residual(0)
+        row_peak(0)
+        scale_residual(1)
+        invert(0)
+        quantise_hid(1)
+        second_product(1)
+        finish(0)
+        row_sizes(1)
+        row_peak(1)
+        invert(1)
+        finish(1)

@@ -29,8 +29,8 @@ def tile_list_two_joined_largest_absgap_rowpeaks_kernel(
         sb = ctx.enter_context(tc.tile_pool(name="sb", bufs=1))
         ps = ctx.enter_context(tc.psum_pool(name="ps", bufs=1))
 
-        def tile(shape, dtype, name):
-            return sb.tile(shape, dtype, name=name, align_bytes=64)
+        def tile(shape, dtype, name, tag=None):
+            return sb.tile(shape, dtype, name=name, tag=tag or name, align_bytes=64)
 
         lists = [tile([P, 8], U16, "list_a"), tile([P, 8], U16, "list_b")]
         list_o = tile([P, 16], U16, "list_o")
@@ -39,6 +39,7 @@ def tile_list_two_joined_largest_absgap_rowpeaks_kernel(
         xo_t = [tile([P, Z], F32, "xo%d" % t) for t in range(PACK)]
         front = [tile([P, 2 * T], F32, "front%d" % h) for h in range(2)]
         back = [[tile([P, T], F32, "back%d_%d" % (h, t)) for t in range(2)] for h in range(2)]
+        window = [[front[h][:, 0:T], front[h][:, T : 2 * T], back[h][0][:], back[h][1][:]] for h in range(2)]
         raw_words = {n: tile([P, R], U32, "raw_words_" + n) for n in ("w", "w2")}
         raw_scales = {n: tile([P, R], U8, "raw_scales_" + n) for n in ("w", "w2")}
         words = {n: tile([P, R], U32, "words_" + n) for n in ("w", "w2")}
@@ -72,10 +73,10 @@ def tile_list_two_joined_largest_absgap_rowpeaks_kernel(
         def load_xo(t):
             load(xo_t[t][:], planes(xo)[:, t * Z : (t + 1) * Z])
 
+        load(fl_t[:], planes(fl))
         load(so_t[:], planes(so))
         load_xo(0)
         load(list_o[:], offs3)
-        load(fl_t[:], planes(fl))
         load_words(raw_words["w2"], w2_words)
         load_scales(raw_scales["w2"], w2_scales, (0, 1))
         load_xo(1)
@@ -88,13 +89,12 @@ def tile_list_two_joined_largest_absgap_rowpeaks_kernel(
         load(lists[0][:], offs)
         load(lists[1][:], offs2)
         load_front(0)
-        load_scales(wb_s, wb_scales, (0, 1))
         load_back(0, 0)
-        load_scales(wb_s, wb_scales, (2, 3))
         load_back(0, 1)
         load_front(1)
         load_back(1, 0)
         load_back(1, 1)
+        load_scales(wb_s, wb_scales, (0, 1, 2, 3))
         load_words(wb_w, wb_words)
         load(rs_t[:].rearrange("p (h n) -> p h n", h=2), rs.rearrange("(h p) n -> p h n", h=2))
 
@@ -108,6 +108,8 @@ def tile_list_two_joined_largest_absgap_rowpeaks_kernel(
                 in_=raw_scales[n][:].rearrange("p (a i t) -> p a t i", t=PACK, i=16),
             )
 
+        neg_fl = tile([P, PACK], F32, "neg_fl")
+        nc.scalar.activation(out=neg_fl[:], in_=fl_t[:], func=ACT.Copy, scale=-1.0)
         u2 = tile([P, J, PACK], BF16, "u2")
 
         def side_plane(t):
@@ -116,7 +118,7 @@ def tile_list_two_joined_largest_absgap_rowpeaks_kernel(
             larger = tile([P, J], F32, "larger%d" % t)
             nc.vector.tensor_tensor(out=larger[:], in0=picked[:], in1=so_t[:, t * J : (t + 1) * J], op=ALU.max)
             nc.vector.tensor_scalar(
-                out=u2[:, :, t], in0=larger[:], scalar1=fl_t[:, t : t + 1], scalar2=-1.0, op0=ALU.mult, op1=ALU.mult
+                out=u2[:, :, t], in0=larger[:], scalar1=neg_fl[:, t : t + 1], scalar2=None, op0=ALU.mult
             )
 
         side_plane(0)
@@ -143,32 +145,30 @@ def tile_list_two_joined_largest_absgap_rowpeaks_kernel(
                     stop=False,
                 )
 
-        u = [tile([P, H, PACK], BF16, "u%d" % h) for h in range(2)]
-        picked = [tile([P, 2, H], F32, "picked%d" % h) for h in range(2)]
+        u = [tile([P, H, PACK], BF16, "u%d" % h, "woven") for h in range(2)]
+        picked = [tile([P, 3, H], F32, "picked%d" % h) for h in range(2)]
         u_w = [tile([P, H], U32, "u_w%d" % h) for h in range(2)]
         u_s = [tile([P, H], U8, "u_s%d" % h) for h in range(2)]
-        hid = [tile([P, H, PACK], BF16, "hid%d" % h) for h in range(2)]
+        hid = [tile([P, H, PACK], BF16, "hid%d" % h, ("picked1", "hid1")[h]) for h in range(2)]
         hid_w = [tile([P, H], U32, "hid_w%d" % h) for h in range(2)]
         hid_s = [tile([P, H], U8, "hid_s%d" % h) for h in range(2)]
         prod = [ps.tile([P, N], F32, name="prod%d" % h) for h in range(2)]
-        resid = [tile([P, N], F32, "resid%d" % h) for h in range(2)]
         size = [tile([P, N], F32, "size%d" % h) for h in range(2)]
+        resid = [tile([P, N], F32, "resid%d" % h, ("picked1", "size0")[h]) for h in range(2)]
         lifted = [tile([P, N], F32, "lifted%d" % h) for h in range(2)]
         denom = [tile([P, 1], F32, "denom%d" % h) for h in range(2)]
         inv = [tile([P, 1], F32, "inv%d" % h) for h in range(2)]
         res = [tile([P, N], F32, "res%d" % h) for h in range(2)]
 
         def pick_front(h):
-            for t in range(2):
-                nc.scalar.activation(
-                    out=picked[h][:, t, :], in_=front[h][:, t * T : (t + 1) * T].indirect(lists[h][:]), func=ACT.Copy
-                )
+            for t in range(3):
+                nc.scalar.activation(out=picked[h][:, t, :], in_=window[h][t].indirect(lists[h][:]), func=ACT.Copy)
 
         def weave_front(h):
-            nc.vector.tensor_copy(out=u[h][:, :, 0:2], in_=picked[h][:].rearrange("p t j -> p j t"))
+            nc.vector.tensor_copy(out=u[h][:, :, 0:3], in_=picked[h][:].rearrange("p t j -> p j t"))
 
-        def pick_back(h, t):
-            nc.vector.tensor_copy(out=u[h][:, :, 2 + t], in_=back[h][t][:].indirect(lists[h][:]))
+        def pick_back(h):
+            nc.vector.tensor_copy(out=u[h][:, :, 3], in_=window[h][3].indirect(lists[h][:]))
 
         def quantise_u(h):
             nc.vector.quantize_mx(
@@ -231,27 +231,25 @@ def tile_list_two_joined_largest_absgap_rowpeaks_kernel(
 
         pick_front(0)
         weave_front(0)
-        pick_back(0, 0)
-        pick_back(0, 1)
+        pick_back(0)
         quantise_u(0)
         first_product(0)
         pick_front(1)
-        magnitude(0)
-        pick_back(1, 0)
         weave_front(1)
-        pick_back(1, 1)
-        quantise_hid(0)
+        pick_back(1)
+        magnitude(0)
         quantise_u(1)
-        second_product(0)
+        quantise_hid(0)
         first_product(1)
-        row_sizes(0)
+        second_product(0)
         magnitude(1)
+        row_sizes(0)
         scale_residual(0)
+        quantise_hid(1)
+        second_product(1)
         row_peak(0)
         scale_residual(1)
         invert(0)
-        quantise_hid(1)
-        second_product(1)
         finish(0)
         row_sizes(1)
         row_peak(1)

@@ -43,7 +43,6 @@ def tile_list_two_joined_largest_absgap_rowpeaks_kernel(
         raw_words = {n: tile([P, R], U32, "raw_words_" + n) for n in ("w", "w2")}
         raw_scales = {n: tile([P, R], U8, "raw_scales_" + n) for n in ("w", "w2")}
         words = {n: tile([P, R], U32, "words_" + n) for n in ("w", "w2")}
-        scales = {n: tile([P, R], U8, "scales_" + n) for n in ("w", "w2")}
         wb_w = tile([P, N], U32, "wb_w")
         wb_s = tile([P, N], U8, "wb_s")
         rs_t = tile([P, 2 * N], F32, "rs_t")
@@ -57,9 +56,11 @@ def tile_list_two_joined_largest_absgap_rowpeaks_kernel(
         def load_words(dst, src):
             load(dst[:].bitcast(I32), src[0].rearrange("p n t -> p (n t)").bitcast(I32))
 
-        def load_scales(dst, src, quadrants):
-            for q in quadrants:
-                load(dst[32 * q : 32 * q + 4, :].bitcast(I32), src[0, 4 * q : 4 * q + 4, :].bitcast(I32))
+        def load_scales(queue, dst, src):
+            for q in range(4):
+                queue.dma_start(
+                    out=dst[32 * q : 32 * q + 4, :].bitcast(I32), in_=src[0, 4 * q : 4 * q + 4, :].bitcast(I32)
+                )
 
         def planes(x):
             return x.rearrange("(p t) c -> p (t c)", t=PACK)
@@ -73,20 +74,19 @@ def tile_list_two_joined_largest_absgap_rowpeaks_kernel(
         def load_xo(t):
             load(xo_t[t][:], planes(xo)[:, t * Z : (t + 1) * Z])
 
-        load(fl_t[:], planes(fl))
+        load_scales(nc.gpsimd, raw_scales["w2"], w2_scales)
+        load_scales(nc.gpsimd, raw_scales["w"], w_scales)
+
         load(so_t[:], planes(so))
         load_xo(0)
+        load(fl_t[:], planes(fl))
         load(list_o[:], offs3)
         load_words(raw_words["w2"], w2_words)
-        load_scales(raw_scales["w2"], w2_scales, (0, 1))
         load_xo(1)
-        load_scales(raw_scales["w2"], w2_scales, (2, 3))
         load_words(raw_words["w"], w_words)
-        load_scales(raw_scales["w"], w_scales, (0, 1))
         load_xo(2)
-        load_scales(raw_scales["w"], w_scales, (2, 3))
-        load_xo(3)
         load(lists[0][:], offs)
+        load_xo(3)
         load(lists[1][:], offs2)
         load_front(0)
         load_back(0, 0)
@@ -94,15 +94,20 @@ def tile_list_two_joined_largest_absgap_rowpeaks_kernel(
         load_front(1)
         load_back(1, 0)
         load_back(1, 1)
-        load_scales(wb_s, wb_scales, (0, 1, 2, 3))
         load_words(wb_w, wb_words)
+        load_scales(nc.sync, wb_s, wb_scales)
         load(rs_t[:].rearrange("p (h n) -> p h n", h=2), rs.rearrange("(h p) n -> p h n", h=2))
 
-        def deal(n):
+        scales = {}
+
+        def deal_words(n):
             nc.vector.tensor_copy(
                 out=words[n][:].rearrange("p (t a i) -> p a t i", t=PACK, i=4),
                 in_=raw_words[n][:].rearrange("p (a i t) -> p a t i", t=PACK, i=4),
             )
+
+        def deal_scales(n, tag):
+            scales.update({n: tile([P, R], U8, "scales_" + n, tag)})
             nc.vector.tensor_copy(
                 out=scales[n][:].rearrange("p (t a i) -> p a t i", t=PACK, i=16),
                 in_=raw_scales[n][:].rearrange("p (a i t) -> p a t i", t=PACK, i=16),
@@ -122,10 +127,11 @@ def tile_list_two_joined_largest_absgap_rowpeaks_kernel(
             )
 
         side_plane(0)
-        deal("w2")
+        deal_words("w2")
         side_plane(1)
-        deal("w")
+        deal_words("w")
         side_plane(2)
+        deal_scales("w2", "larger2")
         side_plane(3)
 
         u2_w = tile([P, J], U32, "u2_w")
@@ -232,6 +238,7 @@ def tile_list_two_joined_largest_absgap_rowpeaks_kernel(
         pick_front(0)
         weave_front(0)
         pick_back(0)
+        deal_scales("w", "picked0")
         quantise_u(0)
         first_product(0)
         pick_front(1)

@@ -38,8 +38,8 @@ def tile_list_two_joined_largest_absgap_rowpeaks_kernel(
         so_t = tile([P, PACK * J], F32, "so_t")
         xo_t = [tile([P, Z], F32, "xo%d" % t) for t in range(PACK)]
         front = [tile([P, 2 * T], F32, "front%d" % h) for h in range(2)]
-        back = [[tile([P, T], F32, "back%d_%d" % (h, t)) for t in range(2)] for h in range(2)]
-        window = [[front[h][:, 0:T], front[h][:, T : 2 * T], back[h][0][:], back[h][1][:]] for h in range(2)]
+        back = [tile([P, 2 * T], F32, "back%d" % h) for h in range(2)]
+        window = [[x[:, t * T : (t + 1) * T] for x in (front[h], back[h]) for t in range(2)] for h in range(2)]
         raw_words = {n: tile([P, R], U32, "raw_words_" + n) for n in ("w", "w2")}
         raw_scales = {n: tile([P, R], U8, "raw_scales_" + n) for n in ("w", "w2")}
         words = {n: tile([P, R], U32, "words_" + n) for n in ("w", "w2")}
@@ -47,7 +47,7 @@ def tile_list_two_joined_largest_absgap_rowpeaks_kernel(
         wb_s = tile([P, N], U8, "wb_s")
         rs_t = tile([P, 2 * N], F32, "rs_t")
 
-        for plane in (raw_scales["w2"], raw_scales["w"], wb_s):
+        for plane in (raw_scales["w"], raw_scales["w2"], wb_s):
             nc.vector.memset(plane[:].bitcast(I32), 0)
 
         def load(dst, src):
@@ -56,8 +56,8 @@ def tile_list_two_joined_largest_absgap_rowpeaks_kernel(
         def load_words(dst, src):
             load(dst[:].bitcast(I32), src[0].rearrange("p n t -> p (n t)").bitcast(I32))
 
-        def load_scales(queue, dst, src):
-            for q in range(4):
+        def load_scales(queue, dst, src, quadrants):
+            for q in quadrants:
                 queue.dma_start(
                     out=dst[32 * q : 32 * q + 4, :].bitcast(I32), in_=src[0, 4 * q : 4 * q + 4, :].bitcast(I32)
                 )
@@ -68,34 +68,34 @@ def tile_list_two_joined_largest_absgap_rowpeaks_kernel(
         def load_front(h):
             load(front[h][:], planes((xa, xb)[h])[:, 0 : 2 * T])
 
-        def load_back(h, t):
-            load(back[h][t][:], planes((xa, xb)[h])[:, (2 + t) * T : (3 + t) * T])
+        def load_back(h, first, last):
+            load(back[h][:, (first - 2) * T : (last - 2) * T], planes((xa, xb)[h])[:, first * T : last * T])
 
         def load_xo(t):
             load(xo_t[t][:], planes(xo)[:, t * Z : (t + 1) * Z])
 
-        load_scales(nc.gpsimd, raw_scales["w2"], w2_scales)
-        load_scales(nc.gpsimd, raw_scales["w"], w_scales)
+        load_scales(nc.gpsimd, raw_scales["w"], w_scales, range(4))
+        load_scales(nc.gpsimd, wb_s, wb_scales, range(4))
 
-        load(so_t[:], planes(so))
-        load_xo(0)
-        load(fl_t[:], planes(fl))
-        load(list_o[:], offs3)
         load_words(raw_words["w2"], w2_words)
-        load_xo(1)
+        load(fl_t[:], planes(fl))
         load_words(raw_words["w"], w_words)
+        load(so_t[:], planes(so))
+        load(list_o[:], offs3)
+        load_xo(0)
+        load_scales(nc.sync, raw_scales["w2"], w2_scales, (0, 1))
+        load_xo(1)
+        load_scales(nc.sync, raw_scales["w2"], w2_scales, (2, 3))
         load_xo(2)
-        load(lists[0][:], offs)
         load_xo(3)
-        load(lists[1][:], offs2)
+        load(lists[0][:], offs)
         load_front(0)
-        load_back(0, 0)
-        load_back(0, 1)
+        load(lists[1][:], offs2)
+        load_back(0, 2, 4)
         load_front(1)
-        load_back(1, 0)
-        load_back(1, 1)
+        load_back(1, 2, 3)
+        load_back(1, 3, 4)
         load_words(wb_w, wb_words)
-        load_scales(nc.sync, wb_s, wb_scales)
         load(rs_t[:].rearrange("p (h n) -> p h n", h=2), rs.rearrange("(h p) n -> p h n", h=2))
 
         scales = {}
@@ -126,17 +126,19 @@ def tile_list_two_joined_largest_absgap_rowpeaks_kernel(
                 out=u2[:, :, t], in0=larger[:], scalar1=neg_fl[:, t : t + 1], scalar2=None, op0=ALU.mult
             )
 
-        side_plane(0)
         deal_words("w2")
-        side_plane(1)
         deal_words("w")
+        side_plane(0)
+        deal_scales("w2", "larger0")
+        side_plane(1)
         side_plane(2)
-        deal_scales("w2", "larger2")
         side_plane(3)
 
         u2_w = tile([P, J], U32, "u2_w")
         u2_s = tile([P, J], U8, "u2_s")
         nc.vector.quantize_mx(out=u2_w[:].bitcast(E4M3), scales=u2_s[:], in_=u2[:].rearrange("p j t -> p (j t)"))
+
+        deal_scales("w", "u2")
 
         gap = [ps.tile([P, PACK, H], F32, name="gap%d" % h) for h in range(2)]
         for h in range(2):
@@ -152,7 +154,7 @@ def tile_list_two_joined_largest_absgap_rowpeaks_kernel(
                 )
 
         u = [tile([P, H, PACK], BF16, "u%d" % h, "woven") for h in range(2)]
-        picked = [tile([P, 3, H], F32, "picked%d" % h) for h in range(2)]
+        picked = [tile([P, (4, 2)[h], H], F32, "picked%d" % h) for h in range(2)]
         u_w = [tile([P, H], U32, "u_w%d" % h) for h in range(2)]
         u_s = [tile([P, H], U8, "u_s%d" % h) for h in range(2)]
         hid = [tile([P, H, PACK], BF16, "hid%d" % h, ("picked1", "hid1")[h]) for h in range(2)]
@@ -167,14 +169,15 @@ def tile_list_two_joined_largest_absgap_rowpeaks_kernel(
         res = [tile([P, N], F32, "res%d" % h) for h in range(2)]
 
         def pick_front(h):
-            for t in range(3):
+            for t in range((4, 2)[h]):
                 nc.scalar.activation(out=picked[h][:, t, :], in_=window[h][t].indirect(lists[h][:]), func=ACT.Copy)
 
         def weave_front(h):
-            nc.vector.tensor_copy(out=u[h][:, :, 0:3], in_=picked[h][:].rearrange("p t j -> p j t"))
+            nc.scalar.copy(out=u[h][:, :, 0:2], in_=picked[h][:].rearrange("p t j -> p j t"))
 
         def pick_back(h):
-            nc.vector.tensor_copy(out=u[h][:, :, 3], in_=window[h][3].indirect(lists[h][:]))
+            for t in (2, 3):
+                nc.vector.tensor_copy(out=u[h][:, :, t], in_=window[h][t].indirect(lists[h][:]))
 
         def quantise_u(h):
             nc.vector.quantize_mx(
@@ -236,9 +239,9 @@ def tile_list_two_joined_largest_absgap_rowpeaks_kernel(
             nc.sync.dma_start(out=out[h * H : (h + 1) * H, :], in_=res[h][:])
 
         pick_front(0)
-        weave_front(0)
-        pick_back(0)
-        deal_scales("w", "picked0")
+        nc.vector.tensor_copy(
+            out=u[0][:].rearrange("p (c i) t -> p c t i", i=4), in_=picked[0][:].rearrange("p t (c i) -> p c t i", i=4)
+        )
         quantise_u(0)
         first_product(0)
         pick_front(1)

from contextlib import ExitStack

import concourse.mybir as mybir

K, T, J, R, Z, N = 512, 512, 256, 512, 1024, 256
FLOPS = 2 * K * R * J * 2 + 2 * J * R * N

F32 = mybir.dt.float32
BF16 = mybir.dt.bfloat16
I32 = mybir.dt.int32
U32 = mybir.dt.uint32
U16 = mybir.dt.uint16
U8 = mybir.dt.uint8
E4M3 = mybir.dt.float8_e4m3fn_x4
E5M2 = mybir.dt.float8_e5m2_x4
ALU = mybir.AluOpType
ACT = mybir.ActivationFunctionType

P = 128
PACK = 4
H = 128


def tile_list_two_joined_largest_absgap_rowpeaks_kernel(
    tc, xa, xb, w_words, w_scales, xo, fl, so, w2_words, w2_scales, wb_words, wb_scales, rs, offs, offs2, offs3, out
):
    nc = tc.nc
    with ExitStack() as ctx:
        sb = ctx.enter_context(tc.tile_pool(name="sb", bufs=1))
        ps = ctx.enter_context(tc.psum_pool(name="ps", bufs=1))

        def tile(shape, dtype, name, tag=None):
            return sb.tile(shape, dtype, name=name, tag=tag or name, align_bytes=64)

        lists = [tile([P, 8], U16, "list_a"), tile([P, 8], U16, "list_b")]
        list_o = tile([P, 16], U16, "list_o")
        fl_t = tile([P, PACK], F32, "fl_t")
        so_t = tile([P, PACK * J], F32, "so_t")
        xo_t = [tile([P, Z], F32, "xo%d" % t) for t in range(PACK)]
        front = [tile([P, 2 * T], F32, "front%d" % h) for h in range(2)]
        back = [tile([P, 2 * T], F32, "back%d" % h) for h in range(2)]
        window = [[x[:, t * T : (t + 1) * T] for x in (front[h], back[h]) for t in range(2)] for h in range(2)]
        raw_words = {n: tile([P, R], U32, "raw_words_" + n) for n in ("w", "w2")}
        raw_scales = {n: tile([P, R], U8, "raw_scales_" + n) for n in ("w", "w2")}
        words = {n: tile([P, R], U32, "words_" + n) for n in ("w", "w2")}
        wb_w = tile([P, N], U32, "wb_w")
        wb_s = tile([P, N], U8, "wb_s")
        rs_t = tile([P, 2 * N], F32, "rs_t")

        for plane in (raw_scales["w"], raw_scales["w2"], wb_s):
            nc.vector.memset(plane[:].bitcast(I32), 0)

        def load(dst, src):
            nc.sync.dma_start(out=dst, in_=src)

        def load_words(dst, src):
            load(dst[:].bitcast(I32), src[0].rearrange("p n t -> p (n t)").bitcast(I32))

        def load_scales(queue, dst, src, quadrants):
            for q in quadrants:
                queue.dma_start(
                    out=dst[32 * q : 32 * q + 4, :].bitcast(I32), in_=src[0, 4 * q : 4 * q + 4, :].bitcast(I32)
                )

        def planes(x):
            return x.rearrange("(p t) c -> p (t c)", t=PACK)

        def load_front(h):
            load(front[h][:], planes((xa, xb)[h])[:, 0 : 2 * T])

        def load_back(h, first, last):
            load(back[h][:, (first - 2) * T : (last - 2) * T], planes((xa, xb)[h])[:, first * T : last * T])

        def load_xo(t):
            load(xo_t[t][:], planes(xo)[:, t * Z : (t + 1) * Z])

        load_scales(nc.gpsimd, raw_scales["w"], w_scales, range(4))
        load_scales(nc.gpsimd, wb_s, wb_scales, range(4))

        load_words(raw_words["w2"], w2_words)
        load(fl_t[:], planes(fl))
        load_words(raw_words["w"], w_words)
        load(so_t[:], planes(so))
        load(list_o[:], offs3)
        load_xo(0)
        load_scales(nc.sync, raw_scales["w2"], w2_scales, (0, 1))
        load_xo(1)
        load_scales(nc.sync, raw_scales["w2"], w2_scales, (2, 3))
        load_xo(2)
        load_xo(3)
        load(lists[0][:], offs)
        load_front(0)
        load(lists[1][:], offs2)
        load_back(0, 2, 4)
        load_front(1)
        load_back(1, 2, 3)
        load_back(1, 3, 4)
        load_words(wb_w, wb_words)
        load(rs_t[:].rearrange("p (h n) -> p h n", h=2), rs.rearrange("(h p) n -> p h n", h=2))

        scales = {}

        def deal_words(n):
            nc.vector.tensor_copy(
                out=words[n][:].rearrange("p (t a i) -> p a t i", t=PACK, i=4),
                in_=raw_words[n][:].rearrange("p (a i t) -> p a t i", t=PACK, i=4),
            )

        def deal_scales(n, tag):
            scales.update({n: tile([P, R], U8, "scales_" + n, tag)})
            nc.vector.tensor_copy(
                out=scales[n][:].rearrange("p (t a i) -> p a t i", t=PACK, i=16),
                in_=raw_scales[n][:].rearrange("p (a i t) -> p a t i", t=PACK, i=16),
            )

        neg_fl = tile([P, PACK], F32, "neg_fl")
        nc.scalar.activation(out=neg_fl[:], in_=fl_t[:], func=ACT.Copy, scale=-1.0)
        u2 = tile([P, J, PACK], BF16, "u2")

        def side_plane(t):
            picked = tile([P, J], F32, "picked_o%d" % t)
            nc.scalar.activation(out=picked[:], in_=xo_t[t][:].indirect(list_o[:]), func=ACT.Copy)
            larger = tile([P, J], F32, "larger%d" % t)
            nc.vector.tensor_tensor(out=larger[:], in0=picked[:], in1=so_t[:, t * J : (t + 1) * J], op=ALU.max)
            nc.vector.tensor_scalar(
                out=u2[:, :, t], in0=larger[:], scalar1=neg_fl[:, t : t + 1], scalar2=None, op0=ALU.mult
            )

        deal_words("w2")
        deal_words("w")
        side_plane(0)
        deal_scales("w2", "larger0")
        side_plane(1)
        side_plane(2)
        side_plane(3)

        u2_w = tile([P, J], U32, "u2_w")
        u2_s = tile([P, J], U8, "u2_s")
        nc.vector.quantize_mx(out=u2_w[:].bitcast(E4M3), scales=u2_s[:], in_=u2[:].rearrange("p j t -> p (j t)"))

        deal_scales("w", "u2")

        gap = [ps.tile([P, PACK, H], F32, name="gap%d" % h) for h in range(2)]
        for h in range(2):
            for t in range(PACK):
                nc.tensor.matmul_mx(
                    out=gap[h][:, t, :],
                    lhsT=words["w2"][:, t * P : (t + 1) * P].bitcast(E5M2),
                    lhsT_scale=scales["w2"][:, t * P : (t + 1) * P],
                    rhs=u2_w[:, h * H : (h + 1) * H].bitcast(E4M3),
                    rhs_scale=u2_s[:, h * H : (h + 1) * H],
                    start=(t == 0),
                    stop=False,
                )

        u = [tile([P, H, PACK], BF16, "u%d" % h, "woven") for h in range(2)]
        picked = [tile([P, (4, 2)[h], H], F32, "picked%d" % h) for h in range(2)]
        u_w = [tile([P, H], U32, "u_w%d" % h) for h in range(2)]
        u_s = [tile([P, H], U8, "u_s%d" % h) for h in range(2)]
        hid = [tile([P, H, PACK], BF16, "hid%d" % h, ("picked1", "hid1")[h]) for h in range(2)]
        hid_w = [tile([P, H], U32, "hid_w%d" % h) for h in range(2)]
        hid_s = [tile([P, H], U8, "hid_s%d" % h) for h in range(2)]
        prod = [ps.tile([P, N], F32, name="prod%d" % h) for h in range(2)]
        size = [tile([P, N], F32, "size%d" % h) for h in range(2)]
        resid = [tile([P, N], F32, "resid%d" % h, ("picked1", "size0")[h]) for h in range(2)]
        lifted = [tile([P, N], F32, "lifted%d" % h) for h in range(2)]
        denom = [tile([P, 1], F32, "denom%d" % h) for h in range(2)]
        inv = [tile([P, 1], F32, "inv%d" % h) for h in range(2)]
        res = [tile([P, N], F32, "res%d" % h) for h in range(2)]

        def pick_front(h):
            for t in range((4, 2)[h]):
                nc.scalar.activation(out=picked[h][:, t, :], in_=window[h][t].indirect(lists[h][:]), func=ACT.Copy)

        def weave_front(h):
            nc.scalar.copy(out=u[h][:, :, 0:2], in_=picked[h][:].rearrange("p t j -> p j t"))

        def pick_back(h):
            for t in (2, 3):
                nc.vector.tensor_copy(out=u[h][:, :, t], in_=window[h][t].indirect(lists[h][:]))

        def quantise_u(h):
            nc.vector.quantize_mx(
                out=u_w[h][:].bitcast(E5M2), scales=u_s[h][:], in_=u[h][:].rearrange("p j t -> p (j t)")
            )

        def first_product(h):
            for t in range(PACK):
                nc.tensor.matmul_mx(
                    out=gap[h][:, t, :],
                    lhsT=words["w"][:, t * P : (t + 1) * P].bitcast(E5M2),
                    lhsT_scale=scales["w"][:, t * P : (t + 1) * P],
                    rhs=u_w[h][:].bitcast(E5M2),
                    rhs_scale=u_s[h][:],
                    start=False,
                    stop=(t == PACK - 1),
                )

        def magnitude(h):
            nc.scalar.activation(out=hid[h][:], in_=gap[h][:].rearrange("p t j -> p j t"), func=ACT.Abs)

        def quantise_hid(h):
            nc.vector.quantize_mx(
                out=hid_w[h][:].bitcast(E5M2), scales=hid_s[h][:], in_=hid[h][:].rearrange("p j t -> p (j t)")
            )

        def second_product(h):
            nc.tensor.matmul_mx(
                out=prod[h][:],
                lhsT=hid_w[h][:].bitcast(E5M2),
                lhsT_scale=hid_s[h][:],
                rhs=wb_w[:].bitcast(E4M3),
                rhs_scale=wb_s[:],
                start=True,
                stop=True,
            )

        def scale_residual(h):
            nc.vector.tensor_scalar(
                out=resid[h][:], in0=rs_t[:, h * N : (h + 1) * N], scalar1=0.3, scalar2=None, op0=ALU.mult
            )

        def row_sizes(h):
            nc.scalar.activation(out=size[h][:], in_=prod[h][:], func=ACT.Abs)

        def row_peak(h):
            nc.vector.tensor_scalar(
                out=lifted[h][:], in0=size[h][:], scalar1=0.2, scalar2=None, op0=ALU.add, op1=ALU.max,
                accum_out=denom[h][:],
            )

        def invert(h):
            nc.vector.reciprocal(out=inv[h][:], in_=denom[h][:])

        def finish(h):
            nc.vector.scalar_tensor_tensor(
                out=res[h][:], in0=prod[h][:], scalar=inv[h][:], in1=resid[h][:], op0=ALU.mult, op1=ALU.add
            )
            nc.sync.dma_start(out=out[h * H : (h + 1) * H, :], in_=res[h][:])

        pick_front(0)
        nc.vector.tensor_copy(
            out=u[0][:].rearrange("p (c i) t -> p c t i", i=4), in_=picked[0][:].rearrange("p t (c i) -> p c t i", i=4)
        )
        quantise_u(0)
        first_product(0)
        pick_front(1)
        weave_front(1)
        pick_back(1)
        magnitude(0)
        quantise_u(1)
        quantise_hid(0)
        first_product(1)
        second_product(0)
        magnitude(1)
        row_sizes(0)
        scale_residual(0)
        quantise_hid(1)
        second_product(1)
        row_peak(0)
        scale_residual(1)
        invert(0)
        finish(0)
        row_sizes(1)
        row_peak(1)
        invert(1)
        finish(1)
